import numpy as np
import ml_dtypes


def mxq(x, axis, fmt="e4m3"):
    dtype, down = {"e4m3": (ml_dtypes.float8_e4m3fn, 7), "e5m2": (ml_dtypes.float8_e5m2, 14)}[fmt]
    v = np.moveaxis(np.asarray(x, np.float32).astype(ml_dtypes.bfloat16).astype(np.float64), axis, -1)
    blocks = v.reshape(v.shape[:-1] + (-1, 32))
    amax = np.abs(blocks).max(-1, keepdims=True)
    byte = np.maximum(np.where(amax > 0, np.frexp(amax)[1] - 1 + 127, 0) - down, 1)
    scale = np.exp2(byte - 127.0)
    codes = (blocks / scale).astype(np.float32).astype(dtype).astype(np.float64)
    return np.moveaxis((codes * scale).reshape(v.shape), -1, axis)


WIDE = False


def mx_kscale(k):
    if not WIDE:
        return np.ones(k)
    levels = np.array([10, -10, 5, -5, 0])
    if k % 512:
        return np.exp2(np.random.permutation(np.resize(levels, k // 32))).repeat(32)
    a = np.empty((k // 512, 16))
    for p in range(k // 512):
        a[p, :8] = np.random.permutation(np.resize(levels, 8))
        for g in range(8):
            far = levels[np.abs(levels - a[p, g]) >= 10]
            a[p, g + 8] = far[np.random.randint(len(far))]
    return np.exp2(a.ravel()).repeat(32)


def f64(x):
    return np.asarray(x).astype(np.float64)


def striped(idx):
    return np.tile(idx.reshape(-1, 16).T, (8, 1)).astype(np.uint16)


def unstriped(offs):
    return offs[:16].T.reshape(-1).astype(np.int64)


def pack_weight(w):
    k, n = w.shape
    w = f64(np.asarray(w, np.float32).astype(ml_dtypes.bfloat16)).reshape(k // 32, 32, n)
    amax = np.abs(w).max(1)
    byte = np.clip(np.where(amax > 0, np.frexp(amax)[1] - 1 + 127 - 7, 1), 1, 254)
    scaled = (w * np.exp2(127.0 - byte)[:, None, :]).reshape(k, n).astype(np.float32)
    words = np.ascontiguousarray(scaled.reshape(k // 512, 128, 4, n).transpose(0, 1, 3, 2)).astype(ml_dtypes.float8_e4m3fn).view(np.uint8)
    return words, np.ascontiguousarray(byte.astype(np.uint8).reshape(k // 512, 16, n))


def unpack_weight(words, scales):
    g, p, n, _ = words.shape
    vals = np.ascontiguousarray(words).view(ml_dtypes.float8_e4m3fn).astype(np.float64) * np.repeat(np.exp2(scales.astype(np.float64) - 127.0), 8, axis=1)[..., None]
    return vals.transpose(0, 1, 3, 2).reshape(g * 512, n)


K, T, S, V, D = 512, 1024, 512, 512, 8


def setup_inputs():
    n = np.random.standard_normal
    s = mx_kscale(K)[:, None]
    packed_xT = pack_weight(n((K, T)) * s)
    packed_eT = pack_weight(n((K, T)) * s)
    return {
        "x_words": packed_xT[0],
        "x_scales": packed_xT[1],
        "e_words": packed_eT[0],
        "e_scales": packed_eT[1],
        "hT": (n((K, V)) / np.sqrt(K) / s).astype(np.float32),
        "gT": (n((K, V)) / np.sqrt(K) / s).astype(np.float32),
        "lr": (np.random.uniform(0.3, 1.0, (V, 1))).astype(np.float32),
        "offs": striped(np.random.permutation(T)[:S]),
    }


def reference(x_words, x_scales, e_words, e_scales, hT, gT, lr, offs):
    hTq = mxq(f64(hT), 0, "e4m3")
    xq = unpack_weight(x_words, x_scales)[:, unstriped(offs)]
    y = hTq.T @ xq
    gTq = mxq(f64(gT), 0, "e4m3")
    e_offs = unpack_weight(e_words, e_scales)[:, unstriped(offs)]
    z = gTq.T @ e_offs
    p = f64(lr) * (y * z)
    return p.reshape(len(p), -1, D).sum(axis=2)

@@ -1,0 +1,118 @@
+from contextlib import ExitStack
+
+import concourse.mybir as mybir
+
+F32 = mybir.dt.float32
+BF16 = mybir.dt.bfloat16
+I32 = mybir.dt.int32
+U32 = mybir.dt.uint32
+U16 = mybir.dt.uint16
+U8 = mybir.dt.uint8
+FP8X4 = mybir.dt.float8_e4m3fn_x4
+MULT = mybir.AluOpType.mult
+ADD = mybir.AluOpType.add
+
+P = 128
+K = 512
+T = 1024
+S = 512
+V = 512
+D = 8
+PACK = 4
+NT = V // P
+FLOPS = 2 * 2 * K * V * S
+
+
+def tile_picked_yghost_sum_p_kernel(tc, x_words, x_scales, e_words, e_scales, hT, gT, lr, offs, out):
+    nc = tc.nc
+    with ExitStack() as ctx:
+        keep = ctx.enter_context(tc.tile_pool(name="keep", bufs=1))
+        psum = ctx.enter_context(tc.psum_pool(name="psum", bufs=1))
+
+        offsets = keep.tile([P, S // 16], U16, name="offsets")
+        nc.sync.dma_start(offsets[:], offs)
+
+        def load_words(name, words):
+            table = keep.tile([P, T], I32, name=name, align_bytes=64)
+            nc.sync.dma_start(table[:], words[0].rearrange("p n t -> p (n t)").bitcast(I32))
+            return table
+
+        def load_scales(name, scales, clear):
+            table = keep.tile([P, T], U8, name=name, align_bytes=64)
+            clear.memset(table[:].bitcast(I32), 0)
+            for q in range(4):
+                nc.scalar.dma_start(table[32 * q : 32 * q + 4, :].bitcast(I32), scales[0, 4 * q : 4 * q + 4, :].bitcast(I32))
+            return table
+
+        def load_cols(name, src, c0, width):
+            raw = keep.tile([P, PACK, width], F32, name=name, align_bytes=64)
+            nc.sync.dma_start(raw[:], src[:, c0 : c0 + width].rearrange("(p j) w -> p j w", j=PACK))
+            return raw
+
+        def gather(name, table, dtype):
+            got = keep.tile([P, S], dtype, name=name, align_bytes=64)
+            nc.vector.tensor_copy(got[:], table.indirect(offsets[:]))
+            return got
+
+        def interleave(name, raw, width):
+            grouped = keep.tile([P, width * PACK], BF16, name=name, align_bytes=64)
+            nc.scalar.copy(
+                grouped[:].rearrange("p (c i t) -> p c t i", i=4, t=PACK),
+                raw[:].rearrange("p t (c i) -> p c t i", i=4),
+            )
+            return grouped
+
+        def quantize(name, grouped, width):
+            codes = keep.tile([P, width], U32, name=name + "_codes", align_bytes=64)
+            scales = keep.tile([P, width], U8, name=name + "_scales", align_bytes=64)
+            nc.vector.quantize_mx(out=codes[:].bitcast(FP8X4), scales=scales[:], in_=grouped[:])
+            return codes, scales
+
+        def product(name, codes, scales, c0, words, bytes_):
+            acc = psum.tile([P, S], F32, name=name)
+            nc.tensor.matmul_mx(
+                out=acc[:],
+                lhsT=codes[:, c0 : c0 + P].bitcast(FP8X4),
+                lhsT_scale=scales[:, c0 : c0 + P],
+                rhs=words[:].bitcast(FP8X4),
+                rhs_scale=bytes_[:],
+                start=True,
+                stop=True,
+            )
+            return acc
+
+        xs_table = load_scales("xs_table", x_scales, nc.vector)
+        xw_table = load_words("xw_table", x_words)
+        h_raw = [load_cols("h_raw0", hT, 0, 256)]
+        es_table = load_scales("es_table", e_scales, nc.gpsimd)
+        ew_table = load_words("ew_table", e_words)
+        h_raw.append(load_cols("h_raw1", hT, 256, 256))
+        g_raw = [load_cols("g_raw%d" % i, gT, i * P, P) for i in range(NT)]
+        lr_cols = keep.tile([P, NT], F32, name="lr_cols")
+        with nc.allow_non_contiguous_dma(reason="one step size to a partition"):
+            nc.sync.dma_start(lr_cols[:], lr.rearrange("(c p) o -> p (c o)", p=P))
+
+        xs = gather("xs", xs_table[:], U8)
+        xw = gather("xw", xw_table[:].bitcast(U32), U32)
+        es = gather("es", es_table[:], U8)
+        y_sb = []
+
+        def y_half(u):
+            codes, scales = quantize("h%d" % u, interleave("h_grouped%d" % u, h_raw[u], 256), 256)
+            for i in range(2):
+                acc = product("y%d" % (2 * u + i), codes, scales, i * P, xw, xs)
+                sb = keep.tile([P, S], F32, name="y_sb%d" % (2 * u + i))
+                nc.scalar.copy(sb[:], acc[:])
+                y_sb.append(sb)
+
+        y_half(0)
+        ew = gather("ew", ew_table[:].bitcast(U32), U32)
+        y_half(1)
+        for i in range(NT):
+            codes, scales = quantize("g%d" % i, interleave("g_grouped%d" % i, g_raw[i], P), P)
+            acc = product("z%d" % i, codes, scales, 0, ew, es)
+            prod = keep.tile([P, S], F32, name="prod%d" % i)
+            nc.vector.scalar_tensor_tensor(prod[:], acc[:], lr_cols[:, i : i + 1], y_sb[i][:], MULT, MULT)
+            sums = keep.tile([P, S // D], F32, name="sums%d" % i)
+            nc.vector.tensor_reduce(sums[:], prod[:].rearrange("p (v d) -> p v d", d=D), mybir.AxisListType.X, ADD)
+            nc.sync.dma_start(out[i * P : (i + 1) * P, :], sums[:])

@@ -20,6 +20,7 @@ V = 512
 D = 8
 PACK = 4
 NT = V // P
+HALF = V // 2
 FLOPS = 2 * 2 * K * V * S
 
 
@@ -29,46 +30,59 @@ def tile_picked_yghost_sum_p_kernel(tc, x_words, x_scales, e_words, e_scales, hT
         keep = ctx.enter_context(tc.tile_pool(name="keep", bufs=1))
         psum = ctx.enter_context(tc.psum_pool(name="psum", bufs=1))
 
-        offsets = keep.tile([P, S // 16], U16, name="offsets")
+        def sbuf(shape, dtype, name, over=None):
+            return keep.tile(shape, dtype, name=name, tag=over or name, align_bytes=64)
+
+        offsets = sbuf([P, S // 16], U16, "offsets")
         nc.sync.dma_start(offsets[:], offs)
 
         def load_words(name, words):
-            table = keep.tile([P, T], I32, name=name, align_bytes=64)
+            table = sbuf([P, T], I32, name)
             nc.sync.dma_start(table[:], words[0].rearrange("p n t -> p (n t)").bitcast(I32))
             return table
 
-        def load_scales(name, scales, clear):
-            table = keep.tile([P, T], U8, name=name, align_bytes=64)
+        def load_scales(name, scales, clear, queue=nc.sync):
+            table = sbuf([P, T], U8, name)
             clear.memset(table[:].bitcast(I32), 0)
             for q in range(4):
-                nc.scalar.dma_start(table[32 * q : 32 * q + 4, :].bitcast(I32), scales[0, 4 * q : 4 * q + 4, :].bitcast(I32))
+                queue.dma_start(table[32 * q : 32 * q + 4, :].bitcast(I32), scales[0, 4 * q : 4 * q + 4, :].bitcast(I32))
             return table
 
         def load_cols(name, src, c0, width):
-            raw = keep.tile([P, PACK, width], F32, name=name, align_bytes=64)
+            raw = sbuf([P, PACK, width], F32, name)
             nc.sync.dma_start(raw[:], src[:, c0 : c0 + width].rearrange("(p j) w -> p j w", j=PACK))
             return raw
 
-        def gather(name, table, dtype):
-            got = keep.tile([P, S], dtype, name=name, align_bytes=64)
+        def load_lr():
+            cols = sbuf([P, NT], F32, "lr_cols")
+            with nc.allow_non_contiguous_dma(reason="one step size to a partition"):
+                nc.sync.dma_start(cols[:], lr.rearrange("(c p) o -> p (c o)", p=P))
+            return cols
+
+        def gather(name, table, dtype, over=None):
+            got = sbuf([P, S], dtype, name, over)
             nc.vector.tensor_copy(got[:], table.indirect(offsets[:]))
             return got
 
-        def interleave(name, raw, width):
-            grouped = keep.tile([P, width * PACK], BF16, name=name, align_bytes=64)
-            nc.scalar.copy(
-                grouped[:].rearrange("p (c i t) -> p c t i", i=4, t=PACK),
-                raw[:].rearrange("p t (c i) -> p c t i", i=4),
-            )
+        def interleave(name, raw, vector_cols=0):
+            grouped = sbuf([P, HALF * PACK], BF16, name)
+            dst = grouped[:].rearrange("p (c i t) -> p c t i", i=4, t=PACK)
+            src = raw[:].rearrange("p t (c i) -> p c t i", i=4)
+            n = (HALF - vector_cols) // 4
+            if n:
+                nc.scalar.copy(dst[:, :n], src[:, :n])
+            if vector_cols:
+                nc.vector.tensor_copy(dst[:, n:], src[:, n:])
             return grouped
 
-        def quantize(name, grouped, width):
-            codes = keep.tile([P, width], U32, name=name + "_codes", align_bytes=64)
-            scales = keep.tile([P, width], U8, name=name + "_scales", align_bytes=64)
+        def quantize(name, grouped, width, over=None):
+            codes = sbuf([P, width], U32, name + "_codes", over)
+            scales = sbuf([P, width], U8, name + "_scales")
             nc.vector.quantize_mx(out=codes[:].bitcast(FP8X4), scales=scales[:], in_=grouped[:])
             return codes, scales
 
-        def product(name, codes, scales, c0, words, bytes_):
+        def product(name, quantized, c0, words, bytes_):
+            codes, scales = quantized
             acc = psum.tile([P, S], F32, name=name)
             nc.tensor.matmul_mx(
                 out=acc[:],
@@ -81,38 +95,68 @@ def tile_picked_yghost_sum_p_kernel(tc, x_words, x_scales, e_words, e_scales, hT
             )
             return acc
 
+        y_sb = {}
+        z = {}
+        prod = {}
+
+        def products(u, name, quantized, words, bytes_):
+            return [product("%s%d" % (name, 2 * u + i), quantized, i * P, words, bytes_) for i in range(2)]
+
+        def evacuate(u, banks, over=None):
+            pair = sbuf([P, 2, S], F32, "pair%d" % u, over)
+            for i in range(2):
+                nc.scalar.copy(pair[:, i, :], banks[i][:])
+                y_sb[2 * u + i] = pair[:, i, :]
+
+        def multiply(i, over=None):
+            prod[i] = sbuf([P, S], F32, "prod%d" % i, over)
+            nc.vector.scalar_tensor_tensor(prod[i][:], z[i][:], lr_cols[:, i : i + 1], y_sb[i], MULT, MULT)
+
+        def finish(i, over=None):
+            sums = sbuf([P, S // D], F32, "sums%d" % i, over)
+            nc.vector.tensor_reduce(sums[:], prod[i][:].rearrange("p (v d) -> p v d", d=D), mybir.AxisListType.X, ADD)
+            nc.sync.dma_start(out[i * P : (i + 1) * P, :], sums[:])
+
+        def finish_pool(i):
+            part, d = prod[i], D
+            while d > 1:
+                d = d // 2
+                halves = part[:].rearrange("p (v h d) -> p v h d", h=2, d=d)
+                part = sbuf([P, S // D * d], F32, "part%d_%d" % (i, d))
+                nc.gpsimd.tensor_tensor(part[:].rearrange("p (v d) -> p v d", d=d), halves[:, :, 0, :], halves[:, :, 1, :], ADD)
+            nc.sync.dma_start(out[i * P : (i + 1) * P, :], part[:])
+
+        h_raw0 = load_cols("h_raw0", hT, 0, HALF)
         xs_table = load_scales("xs_table", x_scales, nc.vector)
         xw_table = load_words("xw_table", x_words)
-        h_raw = [load_cols("h_raw0", hT, 0, 256)]
+        g_raw0 = load_cols("g_raw0", gT, 0, HALF)
         es_table = load_scales("es_table", e_scales, nc.gpsimd)
         ew_table = load_words("ew_table", e_words)
-        h_raw.append(load_cols("h_raw1", hT, 256, 256))
-        g_raw = [load_cols("g_raw%d" % i, gT, i * P, P) for i in range(NT)]
-        lr_cols = keep.tile([P, NT], F32, name="lr_cols")
-        with nc.allow_non_contiguous_dma(reason="one step size to a partition"):
-            nc.sync.dma_start(lr_cols[:], lr.rearrange("(c p) o -> p (c o)", p=P))
+        lr_cols = load_lr()
+        g_raw1 = load_cols("g_raw1", gT, HALF, HALF)
+        h_raw1 = load_cols("h_raw1", hT, HALF, HALF)
 
+        hg0 = interleave("hg0", h_raw0)
         xs = gather("xs", xs_table[:], U8)
+        h0 = quantize("h0", hg0, HALF, "xs_table")
         xw = gather("xw", xw_table[:].bitcast(U32), U32)
+        gg0 = interleave("gg0", g_raw0)
         es = gather("es", es_table[:], U8)
-        y_sb = []
-
-        def y_half(u):
-            codes, scales = quantize("h%d" % u, interleave("h_grouped%d" % u, h_raw[u], 256), 256)
-            for i in range(2):
-                acc = product("y%d" % (2 * u + i), codes, scales, i * P, xw, xs)
-                sb = keep.tile([P, S], F32, name="y_sb%d" % (2 * u + i))
-                nc.scalar.copy(sb[:], acc[:])
-                y_sb.append(sb)
-
-        y_half(0)
+        g0 = quantize("g0", gg0, HALF, "es_table")
+        evacuate(0, products(0, "y", h0, xw, xs), "g_raw0")
         ew = gather("ew", ew_table[:].bitcast(U32), U32)
-        y_half(1)
-        for i in range(NT):
-            codes, scales = quantize("g%d" % i, interleave("g_grouped%d" % i, g_raw[i], P), P)
-            acc = product("z%d" % i, codes, scales, 0, ew, es)
-            prod = keep.tile([P, S], F32, name="prod%d" % i)
-            nc.vector.scalar_tensor_tensor(prod[:], acc[:], lr_cols[:, i : i + 1], y_sb[i][:], MULT, MULT)
-            sums = keep.tile([P, S // D], F32, name="sums%d" % i)
-            nc.vector.tensor_reduce(sums[:], prod[:].rearrange("p (v d) -> p v d", d=D), mybir.AxisListType.X, ADD)
-            nc.sync.dma_start(out[i * P : (i + 1) * P, :], sums[:])
+        z[0], z[1] = products(0, "z", g0, ew, es)
+        gg1 = interleave("gg1", g_raw1, HALF)
+        g1 = quantize("g1", gg1, HALF)
+        hg1 = interleave("hg1", h_raw1)
+        h1 = quantize("h1", hg1, HALF)
+        evacuate(1, products(1, "z", g1, ew, es), "h_raw1")
+        z[2], z[3] = products(1, "y", h1, xw, xs)
+        multiply(0, "hg1")
+        multiply(1)
+        finish(0)
+        multiply(2)
+        finish(1)
+        multiply(3)
+        finish(2)
+        finish(3)

@@ -10,6 +10,7 @@ U16 = mybir.dt.uint16
 U8 = mybir.dt.uint8
 FP8X4 = mybir.dt.float8_e4m3fn_x4
 MULT = mybir.AluOpType.mult
+COPY = mybir.ActivationFunctionType.Copy
 ADD = mybir.AluOpType.add
 
 P = 128
@@ -41,12 +42,14 @@ def tile_picked_yghost_sum_p_kernel(tc, x_words, x_scales, e_words, e_scales, hT
             nc.sync.dma_start(table[:], words[0].rearrange("p n t -> p (n t)").bitcast(I32))
             return table
 
-        def load_scales(name, scales, clear, queue=nc.sync):
+        def scale_table(name, clear):
             table = sbuf([P, T], U8, name)
             clear.memset(table[:].bitcast(I32), 0)
-            for q in range(4):
-                queue.dma_start(table[32 * q : 32 * q + 4, :].bitcast(I32), scales[0, 4 * q : 4 * q + 4, :].bitcast(I32))
             return table
+
+        def load_scales(table, scales, quadrants):
+            for q in quadrants:
+                nc.sync.dma_start(table[32 * q : 32 * q + 4, :].bitcast(I32), scales[0, 4 * q : 4 * q + 4, :].bitcast(I32))
 
         def load_cols(name, src, c0, width):
             raw = sbuf([P, PACK, width], F32, name)
@@ -56,7 +59,7 @@ def tile_picked_yghost_sum_p_kernel(tc, x_words, x_scales, e_words, e_scales, hT
         def load_lr():
             cols = sbuf([P, NT], F32, "lr_cols")
             with nc.allow_non_contiguous_dma(reason="one step size to a partition"):
-                nc.sync.dma_start(cols[:], lr.rearrange("(c p) o -> p (c o)", p=P))
+                nc.gpsimd.dma_start(cols[:], lr.rearrange("(c p) o -> p (c o)", p=P))
             return cols
 
         def gather(name, table, dtype, over=None):
@@ -105,58 +108,63 @@ def tile_picked_yghost_sum_p_kernel(tc, x_words, x_scales, e_words, e_scales, hT
         def evacuate(u, banks, over=None):
             pair = sbuf([P, 2, S], F32, "pair%d" % u, over)
             for i in range(2):
-                nc.scalar.copy(pair[:, i, :], banks[i][:])
+                nc.scalar.activation(pair[:, i, :], banks[i][:], COPY, scale=lr_cols[:, 2 * u + i : 2 * u + i + 1])
                 y_sb[2 * u + i] = pair[:, i, :]
 
         def multiply(i, over=None):
             prod[i] = sbuf([P, S], F32, "prod%d" % i, over)
-            nc.vector.scalar_tensor_tensor(prod[i][:], z[i][:], lr_cols[:, i : i + 1], y_sb[i], MULT, MULT)
+            nc.vector.tensor_tensor(prod[i][:], z[i][:], y_sb[i], MULT)
 
         def finish(i, over=None):
             sums = sbuf([P, S // D], F32, "sums%d" % i, over)
             nc.vector.tensor_reduce(sums[:], prod[i][:].rearrange("p (v d) -> p v d", d=D), mybir.AxisListType.X, ADD)
             nc.sync.dma_start(out[i * P : (i + 1) * P, :], sums[:])
 
-        def finish_pool(i):
-            part, d = prod[i], D
-            while d > 1:
-                d = d // 2
-                halves = part[:].rearrange("p (v h d) -> p v h d", h=2, d=d)
-                part = sbuf([P, S // D * d], F32, "part%d_%d" % (i, d))
-                nc.gpsimd.tensor_tensor(part[:].rearrange("p (v d) -> p v d", d=d), halves[:, :, 0, :], halves[:, :, 1, :], ADD)
-            nc.sync.dma_start(out[i * P : (i + 1) * P, :], part[:])
+        def halve(dst, src, d):
+            halves = src.rearrange("p (v h d) -> p v h d", h=2, d=d)
+            nc.gpsimd.tensor_tensor(dst.rearrange("p (v d) -> p v d", d=d), halves[:, :, 0, :], halves[:, :, 1, :], ADD)
 
-        h_raw0 = load_cols("h_raw0", hT, 0, HALF)
-        xs_table = load_scales("xs_table", x_scales, nc.vector)
-        xw_table = load_words("xw_table", x_words)
-        g_raw0 = load_cols("g_raw0", gT, 0, HALF)
-        es_table = load_scales("es_table", e_scales, nc.gpsimd)
-        ew_table = load_words("ew_table", e_words)
+        def finish_pool(fours):
+            twos = sbuf([P, S // 2], F32, "twos")
+            halve(twos[:], fours[:], 2)
+            ones = sbuf([P, S // 4], F32, "ones")
+            halve(ones[:], twos[:], 1)
+            nc.scalar.dma_start(out[0:HALF, :].rearrange("(i p) v -> p i v", p=P), ones[:].rearrange("p (i v) -> p i v", i=2))
+
+        xs_table = scale_table("xs_table", nc.vector)
+        es_table = scale_table("es_table", nc.gpsimd)
         lr_cols = load_lr()
+        xw_table = load_words("xw_table", x_words)
+        load_scales(xs_table, x_scales, range(4))
+        h_raw0 = load_cols("h_raw0", hT, 0, HALF)
+        load_scales(es_table, e_scales, range(1))
+        ew_table = load_words("ew_table", e_words)
+        load_scales(es_table, e_scales, range(1, 4))
+        g_raw0 = load_cols("g_raw0", gT, 0, HALF)
         g_raw1 = load_cols("g_raw1", gT, HALF, HALF)
         h_raw1 = load_cols("h_raw1", hT, HALF, HALF)
 
-        hg0 = interleave("hg0", h_raw0)
-        xs = gather("xs", xs_table[:], U8)
-        h0 = quantize("h0", hg0, HALF, "xs_table")
         xw = gather("xw", xw_table[:].bitcast(U32), U32)
-        gg0 = interleave("gg0", g_raw0)
-        es = gather("es", es_table[:], U8)
-        g0 = quantize("g0", gg0, HALF, "es_table")
-        evacuate(0, products(0, "y", h0, xw, xs), "g_raw0")
+        xs = gather("xs", xs_table[:], U8)
+        h0 = quantize("h0", interleave("hg0", h_raw0), HALF)
         ew = gather("ew", ew_table[:].bitcast(U32), U32)
+        es = gather("es", es_table[:], U8)
+        g0 = quantize("g0", interleave("gg0", g_raw0), HALF)
+        gg1 = interleave("gg1", g_raw1)
+        evacuate(0, products(0, "y", h0, xw, xs), "g_raw1")
         z[0], z[1] = products(0, "z", g0, ew, es)
-        gg1 = interleave("gg1", g_raw1, HALF)
+        hg1 = interleave("hg1", h_raw1, HALF)
         g1 = quantize("g1", gg1, HALF)
-        hg1 = interleave("hg1", h_raw1)
         h1 = quantize("h1", hg1, HALF)
-        evacuate(1, products(1, "z", g1, ew, es), "h_raw1")
+        evacuate(1, products(1, "z", g1, ew, es))
         z[2], z[3] = products(1, "y", h1, xw, xs)
-        multiply(0, "hg1")
+        fours = sbuf([P, S], F32, "fours")
+        multiply(0)
+        halve(fours[:, :HALF], prod[0][:], 4)
         multiply(1)
-        finish(0)
+        halve(fours[:, HALF:], prod[1][:], 4)
+        finish_pool(fours)
         multiply(2)
-        finish(1)
         multiply(3)
         finish(2)
         finish(3)

@@ -1,6 +1,7 @@
 from contextlib import ExitStack
 
 import concourse.mybir as mybir
+from concourse.masks import make_identity
 
 F32 = mybir.dt.float32
 BF16 = mybir.dt.bfloat16
@@ -57,9 +58,15 @@ def tile_picked_yghost_sum_p_kernel(tc, x_words, x_scales, e_words, e_scales, hT
             return raw
 
         def load_lr():
+            rows = sbuf([P, P], F32, "lr_rows")
+            nc.gpsimd.memset(rows[:], 0.0)
+            nc.gpsimd.dma_start(rows[0:NT, :], lr.rearrange("(c p) o -> c (p o)", p=P))
+            ident = sbuf([P, P], F32, "ident")
+            make_identity(nc, ident[:])
+            turned = psum.tile([P, P], F32, name="lr_turned", tag="y3")
+            nc.tensor.transpose(turned[:], rows[:], ident[:])
             cols = sbuf([P, NT], F32, "lr_cols")
-            with nc.allow_non_contiguous_dma(reason="one step size to a partition"):
-                nc.gpsimd.dma_start(cols[:], lr.rearrange("(c p) o -> p (c o)", p=P))
+            nc.scalar.copy(cols[:], turned[:, 0:NT])
             return cols
 
         def gather(name, table, dtype, over=None):
@@ -67,15 +74,12 @@ def tile_picked_yghost_sum_p_kernel(tc, x_words, x_scales, e_words, e_scales, hT
             nc.vector.tensor_copy(got[:], table.indirect(offsets[:]))
             return got
 
-        def interleave(name, raw, vector_cols=0):
-            grouped = sbuf([P, HALF * PACK], BF16, name)
-            dst = grouped[:].rearrange("p (c i t) -> p c t i", i=4, t=PACK)
-            src = raw[:].rearrange("p t (c i) -> p c t i", i=4)
-            n = (HALF - vector_cols) // 4
-            if n:
-                nc.scalar.copy(dst[:, :n], src[:, :n])
-            if vector_cols:
-                nc.vector.tensor_copy(dst[:, n:], src[:, n:])
+        def interleave(name, raw, copy, over=None):
+            grouped = sbuf([P, raw.shape[2] * PACK], BF16, name, over)
+            copy(
+                grouped[:].rearrange("p (c i t) -> p c t i", i=4, t=PACK),
+                raw[:].rearrange("p t (c i) -> p c t i", i=4),
+            )
             return grouped
 
         def quantize(name, grouped, width, over=None):
@@ -142,22 +146,24 @@ def tile_picked_yghost_sum_p_kernel(tc, x_words, x_scales, e_words, e_scales, hT
         load_scales(es_table, e_scales, range(1, 4))
         g_raw0 = load_cols("g_raw0", gT, 0, HALF)
         g_raw1 = load_cols("g_raw1", gT, HALF, HALF)
-        h_raw1 = load_cols("h_raw1", hT, HALF, HALF)
+        h_raw2 = load_cols("h_raw2", hT, 2 * P, P)
+        h_raw3 = load_cols("h_raw3", hT, 3 * P, P)
 
         xw = gather("xw", xw_table[:].bitcast(U32), U32)
         xs = gather("xs", xs_table[:], U8)
-        h0 = quantize("h0", interleave("hg0", h_raw0), HALF)
+        h0 = quantize("h0", interleave("hg0", h_raw0, nc.scalar.copy), HALF)
         ew = gather("ew", ew_table[:].bitcast(U32), U32)
         es = gather("es", es_table[:], U8)
-        g0 = quantize("g0", interleave("gg0", g_raw0), HALF)
-        gg1 = interleave("gg1", g_raw1)
+        g0 = quantize("g0", interleave("gg0", g_raw0, nc.scalar.copy), HALF)
+        gg1 = interleave("gg1", g_raw1, nc.scalar.copy)
         evacuate(0, products(0, "y", h0, xw, xs), "g_raw1")
         z[0], z[1] = products(0, "z", g0, ew, es)
-        hg1 = interleave("hg1", h_raw1, HALF)
         g1 = quantize("g1", gg1, HALF)
-        h1 = quantize("h1", hg1, HALF)
+        h2 = quantize("h2", interleave("hg2", h_raw2, nc.vector.tensor_copy), P)
+        h3 = quantize("h3", interleave("hg3", h_raw3, nc.vector.tensor_copy, "gg1"), P)
+        z[2] = product("y2", h2, 0, xw, xs)
         evacuate(1, products(1, "z", g1, ew, es))
-        z[2], z[3] = products(1, "y", h1, xw, xs)
+        z[3] = product("y3", h3, 0, xw, xs)
         fours = sbuf([P, S], F32, "fours")
         multiply(0)
         halve(fours[:, :HALF], prod[0][:], 4)

from contextlib import ExitStack

import concourse.mybir as mybir
from concourse.masks import make_identity

F32 = mybir.dt.float32
BF16 = mybir.dt.bfloat16
I32 = mybir.dt.int32
U32 = mybir.dt.uint32
U16 = mybir.dt.uint16
U8 = mybir.dt.uint8
FP8X4 = mybir.dt.float8_e4m3fn_x4
MULT = mybir.AluOpType.mult
COPY = mybir.ActivationFunctionType.Copy
ADD = mybir.AluOpType.add

P = 128
K = 512
T = 1024
S = 512
V = 512
D = 8
PACK = 4
NT = V // P
HALF = V // 2
FLOPS = 2 * 2 * K * V * S


def tile_picked_yghost_sum_p_kernel(tc, x_words, x_scales, e_words, e_scales, hT, gT, lr, offs, out):
    nc = tc.nc
    with ExitStack() as ctx:
        keep = ctx.enter_context(tc.tile_pool(name="keep", bufs=1))
        psum = ctx.enter_context(tc.psum_pool(name="psum", bufs=1))

        def sbuf(shape, dtype, name, over=None):
            return keep.tile(shape, dtype, name=name, tag=over or name, align_bytes=64)

        offsets = sbuf([P, S // 16], U16, "offsets")
        nc.sync.dma_start(offsets[:], offs)

        def load_words(name, words):
            table = sbuf([P, T], I32, name)
            nc.sync.dma_start(table[:], words[0].rearrange("p n t -> p (n t)").bitcast(I32))
            return table

        def scale_table(name, clear):
            table = sbuf([P, T], U8, name)
            clear.memset(table[:].bitcast(I32), 0)
            return table

        def load_scales(table, scales, quadrants):
            for q in quadrants:
                nc.sync.dma_start(table[32 * q : 32 * q + 4, :].bitcast(I32), scales[0, 4 * q : 4 * q + 4, :].bitcast(I32))

        def load_cols(name, src, c0, width):
            raw = sbuf([P, PACK, width], F32, name)
            nc.sync.dma_start(raw[:], src[:, c0 : c0 + width].rearrange("(p j) w -> p j w", j=PACK))
            return raw

        def load_lr():
            rows = sbuf([P, P], F32, "lr_rows")
            nc.gpsimd.memset(rows[:], 0.0)
            nc.gpsimd.dma_start(rows[0:NT, :], lr.rearrange("(c p) o -> c (p o)", p=P))
            ident = sbuf([P, P], F32, "ident")
            make_identity(nc, ident[:])
            turned = psum.tile([P, P], F32, name="lr_turned", tag="y3")
            nc.tensor.transpose(turned[:], rows[:], ident[:])
            cols = sbuf([P, NT], F32, "lr_cols")
            nc.scalar.copy(cols[:], turned[:, 0:NT])
            return cols

        def gather(name, table, dtype, over=None):
            got = sbuf([P, S], dtype, name, over)
            nc.vector.tensor_copy(got[:], table.indirect(offsets[:]))
            return got

        def interleave(name, raw, copy, over=None):
            grouped = sbuf([P, raw.shape[2] * PACK], BF16, name, over)
            copy(
                grouped[:].rearrange("p (c i t) -> p c t i", i=4, t=PACK),
                raw[:].rearrange("p t (c i) -> p c t i", i=4),
            )
            return grouped

        def quantize(name, grouped, width, over=None):
            codes = sbuf([P, width], U32, name + "_codes", over)
            scales = sbuf([P, width], U8, name + "_scales")
            nc.vector.quantize_mx(out=codes[:].bitcast(FP8X4), scales=scales[:], in_=grouped[:])
            return codes, scales

        def product(name, quantized, c0, words, bytes_):
            codes, scales = quantized
            acc = psum.tile([P, S], F32, name=name)
            nc.tensor.matmul_mx(
                out=acc[:],
                lhsT=codes[:, c0 : c0 + P].bitcast(FP8X4),
                lhsT_scale=scales[:, c0 : c0 + P],
                rhs=words[:].bitcast(FP8X4),
                rhs_scale=bytes_[:],
                start=True,
                stop=True,
            )
            return acc

        y_sb = {}
        z = {}
        prod = {}

        def products(u, name, quantized, words, bytes_):
            return [product("%s%d" % (name, 2 * u + i), quantized, i * P, words, bytes_) for i in range(2)]

        def evacuate(u, banks, over=None):
            pair = sbuf([P, 2, S], F32, "pair%d" % u, over)
            for i in range(2):
                nc.scalar.activation(pair[:, i, :], banks[i][:], COPY, scale=lr_cols[:, 2 * u + i : 2 * u + i + 1])
                y_sb[2 * u + i] = pair[:, i, :]

        def multiply(i, over=None):
            prod[i] = sbuf([P, S], F32, "prod%d" % i, over)
            nc.vector.tensor_tensor(prod[i][:], z[i][:], y_sb[i], MULT)

        def finish(i, over=None):
            sums = sbuf([P, S // D], F32, "sums%d" % i, over)
            nc.vector.tensor_reduce(sums[:], prod[i][:].rearrange("p (v d) -> p v d", d=D), mybir.AxisListType.X, ADD)
            nc.sync.dma_start(out[i * P : (i + 1) * P, :], sums[:])

        def halve(dst, src, d):
            halves = src.rearrange("p (v h d) -> p v h d", h=2, d=d)
            nc.gpsimd.tensor_tensor(dst.rearrange("p (v d) -> p v d", d=d), halves[:, :, 0, :], halves[:, :, 1, :], ADD)

        def finish_pool(fours):
            twos = sbuf([P, S // 2], F32, "twos")
            halve(twos[:], fours[:], 2)
            ones = sbuf([P, S // 4], F32, "ones")
            halve(ones[:], twos[:], 1)
            nc.scalar.dma_start(out[0:HALF, :].rearrange("(i p) v -> p i v", p=P), ones[:].rearrange("p (i v) -> p i v", i=2))

        xs_table = scale_table("xs_table", nc.vector)
        es_table = scale_table("es_table", nc.gpsimd)
        lr_cols = load_lr()
        xw_table = load_words("xw_table", x_words)
        load_scales(xs_table, x_scales, range(4))
        h_raw0 = load_cols("h_raw0", hT, 0, HALF)
        load_scales(es_table, e_scales, range(1))
        ew_table = load_words("ew_table", e_words)
        load_scales(es_table, e_scales, range(1, 4))
        g_raw0 = load_cols("g_raw0", gT, 0, HALF)
        g_raw1 = load_cols("g_raw1", gT, HALF, HALF)
        h_raw2 = load_cols("h_raw2", hT, 2 * P, P)
        h_raw3 = load_cols("h_raw3", hT, 3 * P, P)

        xw = gather("xw", xw_table[:].bitcast(U32), U32)
        xs = gather("xs", xs_table[:], U8)
        h0 = quantize("h0", interleave("hg0", h_raw0, nc.scalar.copy), HALF)
        ew = gather("ew", ew_table[:].bitcast(U32), U32)
        es = gather("es", es_table[:], U8)
        g0 = quantize("g0", interleave("gg0", g_raw0, nc.scalar.copy), HALF)
        gg1 = interleave("gg1", g_raw1, nc.scalar.copy)
        evacuate(0, products(0, "y", h0, xw, xs), "g_raw1")
        z[0], z[1] = products(0, "z", g0, ew, es)
        g1 = quantize("g1", gg1, HALF)
        h2 = quantize("h2", interleave("hg2", h_raw2, nc.vector.tensor_copy), P)
        h3 = quantize("h3", interleave("hg3", h_raw3, nc.vector.tensor_copy, "gg1"), P)
        z[2] = product("y2", h2, 0, xw, xs)
        evacuate(1, products(1, "z", g1, ew, es))
        z[3] = product("y3", h3, 0, xw, xs)
        fours = sbuf([P, S], F32, "fours")
        multiply(0)
        halve(fours[:, :HALF], prod[0][:], 4)
        multiply(1)
        halve(fours[:, HALF:], prod[1][:], 4)
        finish_pool(fours)
        multiply(2)
        multiply(3)
        finish(2)
        finish(3)
